import numpy as np
import ml_dtypes


def mxq(x, axis, fmt="e4m3"):
    dtype, down = {"e4m3": (ml_dtypes.float8_e4m3fn, 7), "e5m2": (ml_dtypes.float8_e5m2, 14)}[fmt]
    v = np.moveaxis(np.asarray(x, np.float32).astype(ml_dtypes.bfloat16).astype(np.float64), axis, -1)
    blocks = v.reshape(v.shape[:-1] + (-1, 32))
    amax = np.abs(blocks).max(-1, keepdims=True)
    byte = np.maximum(np.where(amax > 0, np.frexp(amax)[1] - 1 + 127, 0) - down, 1)
    scale = np.exp2(byte - 127.0)
    codes = (blocks / scale).astype(np.float32).astype(dtype).astype(np.float64)
    return np.moveaxis((codes * scale).reshape(v.shape), -1, axis)


WIDE = False


def mx_kscale(k):
    if not WIDE:
        return np.ones(k)
    levels = np.array([10, -10, 5, -5, 0])
    if k % 512:
        return np.exp2(np.random.permutation(np.resize(levels, k // 32))).repeat(32)
    a = np.empty((k // 512, 16))
    for p in range(k // 512):
        a[p, :8] = np.random.permutation(np.resize(levels, 8))
        for g in range(8):
            far = levels[np.abs(levels - a[p, g]) >= 10]
            a[p, g + 8] = far[np.random.randint(len(far))]
    return np.exp2(a.ravel()).repeat(32)


def f64(x):
    return np.asarray(x).astype(np.float64)


def striped(idx):
    return np.tile(idx.reshape(-1, 16).T, (8, 1)).astype(np.uint16)


def unstriped(offs):
    return offs[:16].T.reshape(-1).astype(np.int64)


def striped8(idx):
    return np.concatenate([x.reshape(-1, 16).T for x in idx]).astype(np.uint16)


def runs(offs, k):
    lists = np.stack([offs[16 * r : 16 * r + 16].T.reshape(-1) for r in range(8)]).astype(np.int64)
    return lists[np.arange(k) % 512 // 64]


def pack_weight(w):
    k, n = w.shape
    w = f64(np.asarray(w, np.float32).astype(ml_dtypes.bfloat16)).reshape(k // 32, 32, n)
    amax = np.abs(w).max(1)
    byte = np.clip(np.where(amax > 0, np.frexp(amax)[1] - 1 + 127 - 7, 1), 1, 254)
    scaled = (w * np.exp2(127.0 - byte)[:, None, :]).reshape(k, n).astype(np.float32)
    words = np.ascontiguousarray(scaled.reshape(k // 512, 128, 4, n).transpose(0, 1, 3, 2)).astype(ml_dtypes.float8_e4m3fn).view(np.uint8)
    return words, np.ascontiguousarray(byte.astype(np.uint8).reshape(k // 512, 16, n))


def unpack_weight(words, scales):
    g, p, n, _ = words.shape
    vals = np.ascontiguousarray(words).view(ml_dtypes.float8_e4m3fn).astype(np.float64) * np.repeat(np.exp2(scales.astype(np.float64) - 127.0), 8, axis=1)[..., None]
    return vals.transpose(0, 1, 3, 2).reshape(g * 512, n)


def relu(v):
    return np.maximum(v, 0.0)

def planes(y):
    n, m = y.shape
    v = y.astype(np.float32).astype(ml_dtypes.bfloat16).astype(np.float64).reshape(n // 32, 32, m)
    top = np.abs(v).max(1)
    byte = np.clip(np.where(top > 0, np.frexp(top)[1] - 1 + 127 - 7, 1), 1, 254)
    codes = (v * np.exp2(127.0 - byte)[:, None, :]).reshape(n, m).astype(np.float32).astype(ml_dtypes.float8_e4m3fn).view(np.uint8)
    words = codes.reshape(n // 512, 128, 4, m).transpose(0, 1, 3, 2)
    return np.ascontiguousarray(words), np.ascontiguousarray(byte.astype(np.uint8).reshape(n // 512, 16, m))


K, T, S, N, G, H = 512, 2048, 512, 512, 2048, 512


def setup_inputs():
    n = np.random.standard_normal
    s = mx_kscale(K)[:, None]
    u = mx_kscale(H)
    packed_xT = pack_weight(n((K, T)) * s)
    packed_dT = pack_weight(n((K, G)) / s)
    packed_w1 = pack_weight(n((H, N)) / np.sqrt(H) / u[:, None])
    return {
        "x_words": packed_xT[0],
        "x_scales": packed_xT[1],
        "d_words": packed_dT[0],
        "d_scales": packed_dT[1],
        "gn": (np.random.uniform(0.5, 1.5, (H, 1)) * u[:, None]).astype(np.float32),
        "w1_words": packed_w1[0],
        "w1_scales": packed_w1[1],
        "offs": striped(np.random.permutation(T)[:S]),
        "kidx": striped8(np.random.randint(0, G, (8, H))),
        "n1": striped8(np.stack([np.random.permutation(S) for _ in range(8)])),
        "n2": striped8(np.stack([np.random.permutation(S) for _ in range(8)])),
    }


def reference(x_words, x_scales, d_words, d_scales, gn, w1_words, w1_scales, offs, kidx, n1, n2):
    d_kidx = unpack_weight(d_words, d_scales)[np.arange(K)[:, None], runs(kidx, K)]
    xq = unpack_weight(x_words, x_scales)[:, unstriped(offs)]
    s = 0.0625 * (d_kidx.T @ xq)
    z = f64(gn) * (relu(s - (0.5 * (np.maximum(s[np.arange(H)[:, None], runs(n1, H)], s[np.arange(H)[:, None], runs(n2, H)])))))
    out_0 = unpack_weight(w1_words, w1_scales).T @ mxq(z, 0, "e4m3")
    return (out_0,) + planes(out_0)

@@ -1,0 +1,216 @@
+from contextlib import ExitStack
+
+import concourse.mybir as mybir
+
+K, T, S, N, G, H = 512, 2048, 512, 512, 2048, 512
+FLOPS = 2 * K * H * S + 2 * H * N * S
+
+F32 = mybir.dt.float32
+BF16 = mybir.dt.bfloat16
+I32 = mybir.dt.int32
+U32 = mybir.dt.uint32
+U16 = mybir.dt.uint16
+U8 = mybir.dt.uint8
+FP8X4 = mybir.dt.float8_e4m3fn_x4
+ALU = mybir.AluOpType
+ACT = mybir.ActivationFunctionType
+
+P = 128
+PACK = 4
+SUB = 128
+CHUNKS = ((0, 256), (256, 128), (384, 128))
+HOLD = {(1, 3): "z_woven0", (2, 2): "rounded0", (2, 3): "z_woven1"}
+
+
+def tile_picked_scoreinh_none_po_kernel(
+    tc, x_words, x_scales, d_words, d_scales, gn, w1_words, w1_scales, offs, kidx, n1, n2, out_0, out_1, out_2
+):
+    nc = tc.nc
+    with ExitStack() as ctx:
+        lists = ctx.enter_context(tc.tile_pool(name="lists", bufs=1))
+        keep = ctx.enter_context(tc.tile_pool(name="keep", bufs=1))
+        psum = ctx.enter_context(tc.psum_pool(name="psum", bufs=1))
+
+        def words_view(ap):
+            return ap[0].rearrange("p c r -> p (c r)").bitcast(I32)
+
+        d_scale_table = keep.tile([P, G], U8, tag="early_a", align_bytes=64)
+        x_scale_table = keep.tile([P, T], U8, tag="early_b", align_bytes=64)
+        placed = keep.tile([P, H + S], U8, align_bytes=64)
+        nc.vector.memset(d_scale_table[:].bitcast(I32), 0)
+        nc.gpsimd.memset(x_scale_table[:].bitcast(I32), 0)
+        nc.gpsimd.memset(placed[:].bitcast(I32), 0)
+
+        kidx_sb = lists.tile([P, H // 16], U16)
+        offs_sb = lists.tile([P, S // 16], U16)
+        n1_sb = lists.tile([P, S // 16], U16)
+        n2_sb = lists.tile([P, S // 16], U16)
+        nc.sync.dma_start(kidx_sb[:], kidx)
+        nc.sync.dma_start(offs_sb[:], offs)
+        nc.scalar.dma_start(d_scale_table[0:P:8, :].bitcast(I32), d_scales[0].bitcast(I32))
+        nc.scalar.dma_start(x_scale_table[0:P:8, :].bitcast(I32), x_scales[0].bitcast(I32))
+        d_table = keep.tile([P, G], I32, align_bytes=64)
+        x_table = keep.tile([P, T], I32, align_bytes=64)
+        nc.sync.dma_start(d_table[:], words_view(d_words))
+        nc.sync.dma_start(n1_sb[:], n1)
+        nc.sync.dma_start(n2_sb[:], n2)
+        nc.sync.dma_start(x_table[:], words_view(x_words))
+        gain = keep.tile([P, PACK], F32)
+        nc.gpsimd.dma_start(gain[:], gn.rearrange("(p t) o -> p (t o)", t=PACK))
+
+        picked_scales = keep.tile([P, H + S], U8, align_bytes=64)
+        nc.vector.tensor_copy(picked_scales[:, 0:H], d_scale_table[:].indirect(kidx_sb[:]))
+        nc.vector.tensor_copy(picked_scales[:, H : H + S], x_scale_table[:].indirect(offs_sb[:]))
+        for q in range(4):
+            queue = nc.scalar if q % 2 else nc.sync
+            queue.dma_start(placed[32 * q : 32 * q + 4, :].bitcast(I32), picked_scales[32 * q : 32 * q + 32 : 8, :].bitcast(I32))
+
+        w1_raw = keep.tile([P, N], I32, tag="early_b", align_bytes=64)
+        nc.sync.dma_start(w1_raw[:], words_view(w1_words))
+        w1_scale_raw = keep.tile([P, N], U8, tag="early_a", align_bytes=64)
+        nc.gpsimd.memset(w1_scale_raw[:].bitcast(I32), 0)
+        for q in range(4):
+            nc.sync.dma_start(w1_scale_raw[32 * q : 32 * q + 4, :].bitcast(I32), w1_scales[0, 4 * q : 4 * q + 4, :].bitcast(I32))
+
+        d_picked = keep.tile([P, H], U32, align_bytes=64)
+        nc.vector.tensor_copy(d_picked[:], d_table[:].bitcast(U32).indirect(kidx_sb[:]))
+        d_codes = keep.tile([P, H], I32, align_bytes=64)
+        nc.vector.tensor_copy(d_codes[:].rearrange("p (t m) -> p t m", t=PACK), d_picked[:].bitcast(I32).rearrange("p (m t) -> p t m", t=PACK))
+        x_codes = keep.tile([P, S], U32, align_bytes=64)
+        d_plane = keep.tile([P, H], U8, align_bytes=64)
+        half = S // 2
+        nc.vector.tensor_copy(x_codes[:, 0:half], x_table[:].bitcast(U32).indirect(offs_sb[:, 0 : half // 16]))
+        nc.vector.tensor_copy(d_plane[:].rearrange("p (t m) -> p t m", t=PACK), placed[:, 0:H].rearrange("p (m t) -> p t m", t=PACK))
+        nc.vector.tensor_copy(x_codes[:, half:S], x_table[:].bitcast(U32).indirect(offs_sb[:, half // 16 : S // 16]))
+
+        scores = []
+        plain = []
+        late = []
+        for t in range(PACK):
+            mcols = slice(t * P, (t + 1) * P)
+            row = keep.tile([P, S], F32, name=f"score{t}")
+            own = keep.tile([P, S], F32, name=f"own{t}")
+            pieces = ((0, half), (half, S)) if t == 0 else ((0, S),)
+            for lo, hi in pieces:
+                bank = psum.tile([P, hi - lo], F32, name=f"score_bank{t}_{lo}", tag=f"bank{t}_{lo}")
+                nc.tensor.matmul_mx(
+                    out=bank[:], lhsT=d_codes[:, mcols].bitcast(FP8X4), lhsT_scale=d_plane[:, mcols],
+                    rhs=x_codes[:, lo:hi].bitcast(FP8X4), rhs_scale=placed[:, H + lo : H + hi], start=True, stop=True,
+                )
+                nc.scalar.activation(row[:, lo:hi], bank[:], ACT.Copy, scale=-0.03125)
+                if lo == 0:
+                    nc.scalar.activation(own[:, 0:half], bank[:, 0:half], ACT.Copy, scale=0.0625)
+                if hi == S:
+                    late.append((own, bank[:, half - lo : S - lo]))
+            plain.append(own)
+            scores.append(row)
+        for own, rest in late:
+            nc.scalar.activation(own[:, half:S], rest, ACT.Copy, scale=0.0625)
+
+        w1_codes = keep.tile([P, N], I32, align_bytes=64)
+        nc.vector.tensor_copy(w1_codes[:].rearrange("p (t m) -> p t m", t=PACK), w1_raw[:].rearrange("p (m t) -> p t m", t=PACK))
+        w1_plane = keep.tile([P, N], U8, align_bytes=64)
+        nc.vector.tensor_copy(w1_plane[:].rearrange("p (t m) -> p t m", t=PACK), w1_scale_raw[:].rearrange("p (m t) -> p t m", t=PACK))
+
+        z_codes = keep.tile([P, S], U32, align_bytes=64)
+        z_plane = keep.tile([P, S], U8, align_bytes=64)
+        out_codes = keep.tile([P, S], U32, align_bytes=64)
+        out_plane = keep.tile([P, S], U8, align_bytes=64)
+        out_rows = out_0.rearrange("(p t) j -> p t j", t=PACK)
+        out_words = words_view(out_1)
+
+        widest = max(w for j0, w in CHUNKS)
+        ring_first = keep.tile([P, 2, widest], F32)
+        ring_second = keep.tile([P, 2, widest], F32)
+        last = len(CHUNKS) - 1
+        z_rows = [keep.tile([P, PACK, w], BF16, name=f"z_rows{c}", align_bytes=64) for c, (j0, w) in enumerate(CHUNKS)]
+        units = [(c, t) for c in range(len(CHUNKS)) for t in range(PACK)]
+        firsts = {}
+        woven = {}
+        rounded = {}
+
+        def span(c):
+            j0, w = CHUNKS[c]
+            return slice(j0, j0 + w), slice(j0 // 16, (j0 + w) // 16), w
+
+        def fetch_first(u):
+            c, t = units[u]
+            cols, entries, w = span(c)
+            if (c, t) in HOLD:
+                firsts[u] = keep.tile([P, w], F32, name=f"held{u}", tag=HOLD[(c, t)], align_bytes=64)[:]
+            else:
+                firsts[u] = ring_first[:, u % 2, 0:w]
+            nc.vector.tensor_tensor(firsts[u], scores[t][:].indirect(n1_sb[:, entries]), plain[t][:, cols], ALU.add)
+
+        def fetch_second(u):
+            c, t = units[u]
+            cols, entries, w = span(c)
+            nc.vector.tensor_tensor(ring_second[:, u % 2, 0:w], scores[t][:].indirect(n2_sb[:, entries]), plain[t][:, cols], ALU.add)
+
+        def combine(u):
+            c, t = units[u]
+            cols, entries, w = span(c)
+            second = ring_second[:, u % 2, 0:w]
+            nc.vector.tensor_tensor(second, firsts[u], second, ALU.min)
+
+        def weigh(u):
+            c, t = units[u]
+            cols, entries, w = span(c)
+            second = ring_second[:, u % 2, 0:w]
+            nc.vector.tensor_scalar(z_rows[c][:, t, :], second, 0.0, gain[:, t : t + 1], ALU.max, ALU.mult)
+            if t == PACK - 1:
+                woven[c] = keep.tile([P, w * PACK], BF16, name=f"z_woven{c}", tag=f"z_woven{c}", align_bytes=64)
+                weave = nc.vector.tensor_copy if c == last else nc.scalar.copy
+                weave(woven[c][:].rearrange("p (c i t) -> p c t i", i=4, t=PACK), z_rows[c][:].rearrange("p t (c i) -> p c t i", i=4))
+
+        def second_product(c):
+            cols, entries, w = span(c)
+            nc.vector.quantize_mx(out=z_codes[:, cols].bitcast(FP8X4), scales=z_plane[:, cols], in_=woven[c][:])
+            result = keep.tile([P, PACK, w], F32, name=f"result{c}")
+            rounded[c] = keep.tile([P, w * PACK], BF16, name=f"rounded{c}", tag=f"rounded{c}", align_bytes=64)
+            for u in range(w // SUB):
+                sub = slice(cols.start + u * SUB, cols.start + (u + 1) * SUB)
+                local = slice(u * SUB, (u + 1) * SUB)
+                groups = ((0, 2), (2, 4)) if c == last else ((0, 4),)
+                for lo, hi in groups:
+                    tag = f"bank{lo // 2}_0" if c == last else f"out_bank{sub.start}"
+                    bank = psum.tile([P, hi - lo, SUB], F32, name=f"out_bank{sub.start}_{lo}", tag=tag)
+                    for t in range(lo, hi):
+                        mcols = slice(t * P, (t + 1) * P)
+                        nc.tensor.matmul_mx(
+                            out=bank[:, t - lo, :], lhsT=w1_codes[:, mcols].bitcast(FP8X4), lhsT_scale=w1_plane[:, mcols],
+                            rhs=z_codes[:, sub].bitcast(FP8X4), rhs_scale=z_plane[:, sub], start=True, stop=True,
+                        )
+                    nc.scalar.copy(result[:, lo:hi, local], bank[:])
+                target = rounded[c][:, u * SUB * PACK : (u + 1) * SUB * PACK]
+                if c == last:
+                    nc.vector.tensor_copy(target.rearrange("p (c i t) -> p c t i", i=4, t=PACK), result[:].rearrange("p t (c i) -> p c t i", i=4))
+                else:
+                    nc.scalar.copy(target.rearrange("p (j t) -> p j t", t=PACK), bank[:].rearrange("p t j -> p j t"))
+            nc.sync.dma_start(out_rows[:, :, cols], result[:])
+
+        def hand_on(c):
+            cols, entries, w = span(c)
+            nc.vector.quantize_mx(out=out_codes[:, cols].bitcast(FP8X4), scales=out_plane[:, cols], in_=rounded[c][:])
+            nc.sync.dma_start(out_words[:, cols], out_codes[:, cols].bitcast(I32))
+
+        for u in range(len(units) + 1):
+            if u < len(units):
+                tag = HOLD.get(units[u], "")
+                if tag.startswith("z_woven"):
+                    second_product(int(tag.replace("z_woven", "")))
+                if tag.startswith("rounded"):
+                    hand_on(int(tag.replace("rounded", "")))
+                fetch_first(u)
+            if u > 0:
+                combine(u - 1)
+            if u < len(units):
+                fetch_second(u)
+            if u > 0:
+                weigh(u - 1)
+        second_product(last)
+        hand_on(last - 1)
+        hand_on(last)
+        for q in range(4):
+            queue = nc.scalar if q % 2 else nc.sync
+            queue.dma_start(out_2[0, 4 * q : 4 * q + 4, :].bitcast(I32), out_plane[32 * q : 32 * q + 4, :].bitcast(I32))

@@ -17,9 +17,14 @@ ACT = mybir.ActivationFunctionType
 
 P = 128
 PACK = 4
+QUADS = 4
+GROUP = 16
+LINE = 4
+SCALE = 0.0625
+HALF = S // 2
 SUB = 128
 CHUNKS = ((0, 256), (256, 128), (384, 128))
-HOLD = {(1, 3): "z_woven0", (2, 2): "rounded0", (2, 3): "z_woven1"}
+QUANTISE_AT = {(c + 1, PACK - 1): c for c in range(len(CHUNKS) - 1)}
 
 
 def tile_picked_scoreinh_none_po_kernel(
@@ -31,186 +36,210 @@ def tile_picked_scoreinh_none_po_kernel(
         keep = ctx.enter_context(tc.tile_pool(name="keep", bufs=1))
         psum = ctx.enter_context(tc.psum_pool(name="psum", bufs=1))
 
-        def words_view(ap):
-            return ap[0].rearrange("p c r -> p (c r)").bitcast(I32)
+        def as_words(dram):
+            return dram[0].rearrange("p c r -> p (c r)").bitcast(I32)
 
-        d_scale_table = keep.tile([P, G], U8, tag="early_a", align_bytes=64)
-        x_scale_table = keep.tile([P, T], U8, tag="early_b", align_bytes=64)
-        placed = keep.tile([P, H + S], U8, align_bytes=64)
-        nc.vector.memset(d_scale_table[:].bitcast(I32), 0)
-        nc.gpsimd.memset(x_scale_table[:].bitcast(I32), 0)
-        nc.gpsimd.memset(placed[:].bitcast(I32), 0)
+        def by_set(dealt):
+            return dealt.rearrange("p (t m) -> p m t", t=PACK)
 
-        kidx_sb = lists.tile([P, H // 16], U16)
-        offs_sb = lists.tile([P, S // 16], U16)
-        n1_sb = lists.tile([P, S // 16], U16)
-        n2_sb = lists.tile([P, S // 16], U16)
+        def by_column(plain):
+            return plain.rearrange("p (m t) -> p m t", t=PACK)
+
+        def weave(copy, woven_out, row_sets):
+            copy(
+                woven_out.rearrange("p (c i t) -> p c t i", i=LINE, t=PACK),
+                row_sets.rearrange("p t (c i) -> p c t i", i=LINE),
+            )
+
+        def entries(lo, hi):
+            return slice(lo // GROUP, hi // GROUP)
+
+        d_scale_table = keep.tile([P, G], U8, tag="d_scales_then_w1_scales", align_bytes=64)
+        x_scale_table = keep.tile([P, T], U8, tag="x_scales_then_w1_words", align_bytes=64)
+        placed_scales = keep.tile([P, H + S], U8, align_bytes=64)
+        nc.gpsimd.memset(d_scale_table[:].bitcast(I32), 0)
+        nc.vector.memset(x_scale_table[:].bitcast(I32), 0)
+        nc.vector.memset(placed_scales[:].bitcast(I32), 0)
+
+        kidx_sb = lists.tile([P, H // GROUP], U16)
+        offs_sb = lists.tile([P, S // GROUP], U16)
+        n1_sb = lists.tile([P, S // GROUP], U16)
+        n2_sb = lists.tile([P, S // GROUP], U16)
         nc.sync.dma_start(kidx_sb[:], kidx)
         nc.sync.dma_start(offs_sb[:], offs)
-        nc.scalar.dma_start(d_scale_table[0:P:8, :].bitcast(I32), d_scales[0].bitcast(I32))
-        nc.scalar.dma_start(x_scale_table[0:P:8, :].bitcast(I32), x_scales[0].bitcast(I32))
-        d_table = keep.tile([P, G], I32, align_bytes=64)
-        x_table = keep.tile([P, T], I32, align_bytes=64)
-        nc.sync.dma_start(d_table[:], words_view(d_words))
         nc.sync.dma_start(n1_sb[:], n1)
         nc.sync.dma_start(n2_sb[:], n2)
-        nc.sync.dma_start(x_table[:], words_view(x_words))
         gain = keep.tile([P, PACK], F32)
-        nc.gpsimd.dma_start(gain[:], gn.rearrange("(p t) o -> p (t o)", t=PACK))
+        nc.sync.dma_start(d_scale_table[0:P:8, :].bitcast(I32), d_scales[0].bitcast(I32))
+        nc.sync.dma_start(gain[:], gn.rearrange("(p t) o -> p (t o)", t=PACK))
+        nc.sync.dma_start(x_scale_table[0:P:8, :].bitcast(I32), x_scales[0].bitcast(I32))
+        d_table = keep.tile([P, G], I32, align_bytes=64)
+        x_table = keep.tile([P, T], I32, align_bytes=64)
+        nc.sync.dma_start(d_table[:], as_words(d_words))
+        nc.sync.dma_start(x_table[:], as_words(x_words))
 
         picked_scales = keep.tile([P, H + S], U8, align_bytes=64)
         nc.vector.tensor_copy(picked_scales[:, 0:H], d_scale_table[:].indirect(kidx_sb[:]))
         nc.vector.tensor_copy(picked_scales[:, H : H + S], x_scale_table[:].indirect(offs_sb[:]))
-        for q in range(4):
+        for q in range(QUADS):
             queue = nc.scalar if q % 2 else nc.sync
-            queue.dma_start(placed[32 * q : 32 * q + 4, :].bitcast(I32), picked_scales[32 * q : 32 * q + 32 : 8, :].bitcast(I32))
+            queue.dma_start(
+                placed_scales[32 * q : 32 * q + 4, :].bitcast(I32),
+                picked_scales[32 * q : 32 * q + 32 : 8, :].bitcast(I32),
+            )
 
-        w1_raw = keep.tile([P, N], I32, tag="early_b", align_bytes=64)
-        nc.sync.dma_start(w1_raw[:], words_view(w1_words))
-        w1_scale_raw = keep.tile([P, N], U8, tag="early_a", align_bytes=64)
-        nc.gpsimd.memset(w1_scale_raw[:].bitcast(I32), 0)
-        for q in range(4):
-            nc.sync.dma_start(w1_scale_raw[32 * q : 32 * q + 4, :].bitcast(I32), w1_scales[0, 4 * q : 4 * q + 4, :].bitcast(I32))
+        w1_table = keep.tile([P, N], I32, tag="x_scales_then_w1_words", align_bytes=64)
+        nc.sync.dma_start(w1_table[:], as_words(w1_words))
+        w1_scale_table = keep.tile([P, N], U8, tag="d_scales_then_w1_scales", align_bytes=64)
+        nc.gpsimd.memset(w1_scale_table[:].bitcast(I32), 0)
+        for q in range(QUADS):
+            nc.sync.dma_start(
+                w1_scale_table[32 * q : 32 * q + 4, :].bitcast(I32), w1_scales[0, 4 * q : 4 * q + 4, :].bitcast(I32)
+            )
 
         d_picked = keep.tile([P, H], U32, align_bytes=64)
         nc.vector.tensor_copy(d_picked[:], d_table[:].bitcast(U32).indirect(kidx_sb[:]))
         d_codes = keep.tile([P, H], I32, align_bytes=64)
-        nc.vector.tensor_copy(d_codes[:].rearrange("p (t m) -> p t m", t=PACK), d_picked[:].bitcast(I32).rearrange("p (m t) -> p t m", t=PACK))
+        nc.vector.tensor_copy(by_set(d_codes[:]), by_column(d_picked[:].bitcast(I32)))
         x_codes = keep.tile([P, S], U32, align_bytes=64)
         d_plane = keep.tile([P, H], U8, align_bytes=64)
-        half = S // 2
-        nc.vector.tensor_copy(x_codes[:, 0:half], x_table[:].bitcast(U32).indirect(offs_sb[:, 0 : half // 16]))
-        nc.vector.tensor_copy(d_plane[:].rearrange("p (t m) -> p t m", t=PACK), placed[:, 0:H].rearrange("p (m t) -> p t m", t=PACK))
-        nc.vector.tensor_copy(x_codes[:, half:S], x_table[:].bitcast(U32).indirect(offs_sb[:, half // 16 : S // 16]))
+        nc.vector.tensor_copy(x_codes[:, 0:HALF], x_table[:].bitcast(U32).indirect(offs_sb[:, entries(0, HALF)]))
+        nc.vector.tensor_copy(by_set(d_plane[:]), by_column(placed_scales[:, 0:H]))
+        nc.vector.tensor_copy(x_codes[:, HALF:S], x_table[:].bitcast(U32).indirect(offs_sb[:, entries(HALF, S)]))
 
-        scores = []
-        plain = []
-        late = []
+        rival, own, second_halves = [], [], []
         for t in range(PACK):
-            mcols = slice(t * P, (t + 1) * P)
-            row = keep.tile([P, S], F32, name=f"score{t}")
-            own = keep.tile([P, S], F32, name=f"own{t}")
-            pieces = ((0, half), (half, S)) if t == 0 else ((0, S),)
-            for lo, hi in pieces:
+            stationary = slice(t * P, (t + 1) * P)
+            rival.append(keep.tile([P, S], F32, name=f"rival{t}"))
+            own.append(keep.tile([P, S], F32, name=f"own{t}"))
+            for lo, hi in ((0, HALF), (HALF, S)) if t == 0 else ((0, S),):
                 bank = psum.tile([P, hi - lo], F32, name=f"score_bank{t}_{lo}", tag=f"bank{t}_{lo}")
                 nc.tensor.matmul_mx(
-                    out=bank[:], lhsT=d_codes[:, mcols].bitcast(FP8X4), lhsT_scale=d_plane[:, mcols],
-                    rhs=x_codes[:, lo:hi].bitcast(FP8X4), rhs_scale=placed[:, H + lo : H + hi], start=True, stop=True,
+                    out=bank[:],
+                    lhsT=d_codes[:, stationary].bitcast(FP8X4),
+                    lhsT_scale=d_plane[:, stationary],
+                    rhs=x_codes[:, lo:hi].bitcast(FP8X4),
+                    rhs_scale=placed_scales[:, H + lo : H + hi],
+                    start=True,
+                    stop=True,
                 )
-                nc.scalar.activation(row[:, lo:hi], bank[:], ACT.Copy, scale=-0.03125)
+                nc.scalar.activation(rival[t][:, lo:hi], bank[:], ACT.Copy, scale=-0.5 * SCALE)
                 if lo == 0:
-                    nc.scalar.activation(own[:, 0:half], bank[:, 0:half], ACT.Copy, scale=0.0625)
+                    nc.scalar.activation(own[t][:, 0:HALF], bank[:, 0:HALF], ACT.Copy, scale=SCALE)
                 if hi == S:
-                    late.append((own, bank[:, half - lo : S - lo]))
-            plain.append(own)
-            scores.append(row)
-        for own, rest in late:
-            nc.scalar.activation(own[:, half:S], rest, ACT.Copy, scale=0.0625)
+                    second_halves.append(bank[:, HALF - lo : S - lo])
+        for t in range(PACK):
+            nc.scalar.activation(own[t][:, HALF:S], second_halves[t], ACT.Copy, scale=SCALE)
 
         w1_codes = keep.tile([P, N], I32, align_bytes=64)
-        nc.vector.tensor_copy(w1_codes[:].rearrange("p (t m) -> p t m", t=PACK), w1_raw[:].rearrange("p (m t) -> p t m", t=PACK))
+        nc.vector.tensor_copy(by_set(w1_codes[:]), by_column(w1_table[:]))
         w1_plane = keep.tile([P, N], U8, align_bytes=64)
-        nc.vector.tensor_copy(w1_plane[:].rearrange("p (t m) -> p t m", t=PACK), w1_scale_raw[:].rearrange("p (m t) -> p t m", t=PACK))
+        nc.vector.tensor_copy(by_set(w1_plane[:]), by_column(w1_scale_table[:]))
 
         z_codes = keep.tile([P, S], U32, align_bytes=64)
         z_plane = keep.tile([P, S], U8, align_bytes=64)
         out_codes = keep.tile([P, S], U32, align_bytes=64)
         out_plane = keep.tile([P, S], U8, align_bytes=64)
         out_rows = out_0.rearrange("(p t) j -> p t j", t=PACK)
-        out_words = words_view(out_1)
+        out_words = as_words(out_1)
 
-        widest = max(w for j0, w in CHUNKS)
-        ring_first = keep.tile([P, 2, widest], F32)
-        ring_second = keep.tile([P, 2, widest], F32)
+        widest = max(width for first_column, width in CHUNKS)
+        ring_n1 = keep.tile([P, 2, widest], F32)
+        ring_n2 = keep.tile([P, 2, widest], F32)
         last = len(CHUNKS) - 1
-        z_rows = [keep.tile([P, PACK, w], BF16, name=f"z_rows{c}", align_bytes=64) for c, (j0, w) in enumerate(CHUNKS)]
-        units = [(c, t) for c in range(len(CHUNKS)) for t in range(PACK)]
-        firsts = {}
-        woven = {}
-        rounded = {}
+        z_sets = [
+            keep.tile([P, PACK, width], BF16, name=f"z_sets{c}", align_bytes=64)
+            for c, (first_column, width) in enumerate(CHUNKS)
+        ]
+        steps = [(c, t) for c in range(len(CHUNKS)) for t in range(PACK)]
+        margin_n1, z_woven, out_woven = {}, {}, {}
 
-        def span(c):
-            j0, w = CHUNKS[c]
-            return slice(j0, j0 + w), slice(j0 // 16, (j0 + w) // 16), w
+        def columns(c):
+            first_column, width = CHUNKS[c]
+            return slice(first_column, first_column + width), width
 
-        def fetch_first(u):
-            c, t = units[u]
-            cols, entries, w = span(c)
-            if (c, t) in HOLD:
-                firsts[u] = keep.tile([P, w], F32, name=f"held{u}", tag=HOLD[(c, t)], align_bytes=64)[:]
+        def fetch_n1(u):
+            c, t = steps[u]
+            cols, width = columns(c)
+            if (c, t) in QUANTISE_AT:
+                tag = f"z_woven{QUANTISE_AT[(c, t)]}"
+                margin_n1[u] = keep.tile([P, width], F32, name=f"margin{u}", tag=tag, align_bytes=64)[:]
             else:
-                firsts[u] = ring_first[:, u % 2, 0:w]
-            nc.vector.tensor_tensor(firsts[u], scores[t][:].indirect(n1_sb[:, entries]), plain[t][:, cols], ALU.add)
+                margin_n1[u] = ring_n1[:, u % 2, 0:width]
+            picked = rival[t][:].indirect(n1_sb[:, entries(cols.start, cols.stop)])
+            nc.vector.tensor_tensor(margin_n1[u], picked, own[t][:, cols], ALU.add)
 
-        def fetch_second(u):
-            c, t = units[u]
-            cols, entries, w = span(c)
-            nc.vector.tensor_tensor(ring_second[:, u % 2, 0:w], scores[t][:].indirect(n2_sb[:, entries]), plain[t][:, cols], ALU.add)
+        def fetch_n2(u):
+            c, t = steps[u]
+            cols, width = columns(c)
+            picked = rival[t][:].indirect(n2_sb[:, entries(cols.start, cols.stop)])
+            nc.vector.tensor_tensor(ring_n2[:, u % 2, 0:width], picked, own[t][:, cols], ALU.add)
 
-        def combine(u):
-            c, t = units[u]
-            cols, entries, w = span(c)
-            second = ring_second[:, u % 2, 0:w]
-            nc.vector.tensor_tensor(second, firsts[u], second, ALU.min)
+        def take_lesser(u):
+            c, t = steps[u]
+            cols, width = columns(c)
+            margin_n2 = ring_n2[:, u % 2, 0:width]
+            nc.vector.tensor_tensor(margin_n2, margin_n1[u], margin_n2, ALU.min)
 
         def weigh(u):
-            c, t = units[u]
-            cols, entries, w = span(c)
-            second = ring_second[:, u % 2, 0:w]
-            nc.vector.tensor_scalar(z_rows[c][:, t, :], second, 0.0, gain[:, t : t + 1], ALU.max, ALU.mult)
+            c, t = steps[u]
+            cols, width = columns(c)
+            lesser = ring_n2[:, u % 2, 0:width]
+            nc.vector.tensor_scalar(z_sets[c][:, t, :], lesser, 0.0, gain[:, t : t + 1], ALU.max, ALU.mult)
             if t == PACK - 1:
-                woven[c] = keep.tile([P, w * PACK], BF16, name=f"z_woven{c}", tag=f"z_woven{c}", align_bytes=64)
-                weave = nc.vector.tensor_copy if c == last else nc.scalar.copy
-                weave(woven[c][:].rearrange("p (c i t) -> p c t i", i=4, t=PACK), z_rows[c][:].rearrange("p t (c i) -> p c t i", i=4))
+                z_woven[c] = keep.tile([P, width * PACK], BF16, name=f"z_woven{c}", tag=f"z_woven{c}", align_bytes=64)
+                weave(nc.vector.tensor_copy if c == last else nc.scalar.copy, z_woven[c][:], z_sets[c][:])
 
         def second_product(c):
-            cols, entries, w = span(c)
-            nc.vector.quantize_mx(out=z_codes[:, cols].bitcast(FP8X4), scales=z_plane[:, cols], in_=woven[c][:])
-            result = keep.tile([P, PACK, w], F32, name=f"result{c}")
-            rounded[c] = keep.tile([P, w * PACK], BF16, name=f"rounded{c}", tag=f"rounded{c}", align_bytes=64)
-            for u in range(w // SUB):
-                sub = slice(cols.start + u * SUB, cols.start + (u + 1) * SUB)
-                local = slice(u * SUB, (u + 1) * SUB)
-                groups = ((0, 2), (2, 4)) if c == last else ((0, 4),)
-                for lo, hi in groups:
-                    tag = f"bank{lo // 2}_0" if c == last else f"out_bank{sub.start}"
-                    bank = psum.tile([P, hi - lo, SUB], F32, name=f"out_bank{sub.start}_{lo}", tag=tag)
-                    for t in range(lo, hi):
-                        mcols = slice(t * P, (t + 1) * P)
+            cols, width = columns(c)
+            nc.vector.quantize_mx(out=z_codes[:, cols].bitcast(FP8X4), scales=z_plane[:, cols], in_=z_woven[c][:])
+            result = keep.tile([P, PACK, width], F32, name=f"result{c}")
+            out_woven[c] = keep.tile([P, width * PACK], BF16, name=f"out_woven{c}", align_bytes=64)
+            for lo in range(0, width, SUB):
+                moving = slice(cols.start + lo, cols.start + lo + SUB)
+                for t_lo, t_hi in ((0, 2), (2, 4)) if c == last else ((0, PACK),):
+                    tag = f"bank{t_lo // 2}_0" if c == last else f"out_bank{moving.start}"
+                    bank = psum.tile([P, t_hi - t_lo, SUB], F32, name=f"out_bank{moving.start}_{t_lo}", tag=tag)
+                    for t in range(t_lo, t_hi):
+                        stationary = slice(t * P, (t + 1) * P)
                         nc.tensor.matmul_mx(
-                            out=bank[:, t - lo, :], lhsT=w1_codes[:, mcols].bitcast(FP8X4), lhsT_scale=w1_plane[:, mcols],
-                            rhs=z_codes[:, sub].bitcast(FP8X4), rhs_scale=z_plane[:, sub], start=True, stop=True,
+                            out=bank[:, t - t_lo, :],
+                            lhsT=w1_codes[:, stationary].bitcast(FP8X4),
+                            lhsT_scale=w1_plane[:, stationary],
+                            rhs=z_codes[:, moving].bitcast(FP8X4),
+                            rhs_scale=z_plane[:, moving],
+                            start=True,
+                            stop=True,
                         )
-                    nc.scalar.copy(result[:, lo:hi, local], bank[:])
-                target = rounded[c][:, u * SUB * PACK : (u + 1) * SUB * PACK]
+                    nc.scalar.copy(result[:, t_lo:t_hi, lo : lo + SUB], bank[:])
+                target = out_woven[c][:, lo * PACK : (lo + SUB) * PACK]
                 if c == last:
-                    nc.vector.tensor_copy(target.rearrange("p (c i t) -> p c t i", i=4, t=PACK), result[:].rearrange("p t (c i) -> p c t i", i=4))
+                    weave(nc.vector.tensor_copy, target, result[:])
                 else:
                     nc.scalar.copy(target.rearrange("p (j t) -> p j t", t=PACK), bank[:].rearrange("p t j -> p j t"))
             nc.sync.dma_start(out_rows[:, :, cols], result[:])
 
         def hand_on(c):
-            cols, entries, w = span(c)
-            nc.vector.quantize_mx(out=out_codes[:, cols].bitcast(FP8X4), scales=out_plane[:, cols], in_=rounded[c][:])
+            cols, width = columns(c)
+            nc.vector.quantize_mx(out=out_codes[:, cols].bitcast(FP8X4), scales=out_plane[:, cols], in_=out_woven[c][:])
             nc.sync.dma_start(out_words[:, cols], out_codes[:, cols].bitcast(I32))
 
-        for u in range(len(units) + 1):
-            if u < len(units):
-                tag = HOLD.get(units[u], "")
-                if tag.startswith("z_woven"):
-                    second_product(int(tag.replace("z_woven", "")))
-                if tag.startswith("rounded"):
-                    hand_on(int(tag.replace("rounded", "")))
-                fetch_first(u)
+        for u in range(len(steps) + 1):
+            if u < len(steps):
+                if steps[u] in QUANTISE_AT:
+                    second_product(QUANTISE_AT[steps[u]])
+                fetch_n1(u)
+            else:
+                hand_on(0)
             if u > 0:
-                combine(u - 1)
-            if u < len(units):
-                fetch_second(u)
+                take_lesser(u - 1)
+            if u < len(steps):
+                fetch_n2(u)
             if u > 0:
                 weigh(u - 1)
         second_product(last)
         hand_on(last - 1)
         hand_on(last)
-        for q in range(4):
+        for q in range(QUADS):
             queue = nc.scalar if q % 2 else nc.sync
             queue.dma_start(out_2[0, 4 * q : 4 * q + 4, :].bitcast(I32), out_plane[32 * q : 32 * q + 4, :].bitcast(I32))

from contextlib import ExitStack

import concourse.mybir as mybir

K, T, S, N, G, H = 512, 2048, 512, 512, 2048, 512
FLOPS = 2 * K * H * S + 2 * H * N * S

F32 = mybir.dt.float32
BF16 = mybir.dt.bfloat16
I32 = mybir.dt.int32
U32 = mybir.dt.uint32
U16 = mybir.dt.uint16
U8 = mybir.dt.uint8
FP8X4 = mybir.dt.float8_e4m3fn_x4
ALU = mybir.AluOpType
ACT = mybir.ActivationFunctionType

P = 128
PACK = 4
QUADS = 4
GROUP = 16
LINE = 4
SCALE = 0.0625
HALF = S // 2
SUB = 128
CHUNKS = ((0, 256), (256, 128), (384, 128))
QUANTISE_AT = {(c + 1, PACK - 1): c for c in range(len(CHUNKS) - 1)}


def tile_picked_scoreinh_none_po_kernel(
    tc, x_words, x_scales, d_words, d_scales, gn, w1_words, w1_scales, offs, kidx, n1, n2, out_0, out_1, out_2
):
    nc = tc.nc
    with ExitStack() as ctx:
        lists = ctx.enter_context(tc.tile_pool(name="lists", bufs=1))
        keep = ctx.enter_context(tc.tile_pool(name="keep", bufs=1))
        psum = ctx.enter_context(tc.psum_pool(name="psum", bufs=1))

        def as_words(dram):
            return dram[0].rearrange("p c r -> p (c r)").bitcast(I32)

        def by_set(dealt):
            return dealt.rearrange("p (t m) -> p m t", t=PACK)

        def by_column(plain):
            return plain.rearrange("p (m t) -> p m t", t=PACK)

        def weave(copy, woven_out, row_sets):
            copy(
                woven_out.rearrange("p (c i t) -> p c t i", i=LINE, t=PACK),
                row_sets.rearrange("p t (c i) -> p c t i", i=LINE),
            )

        def entries(lo, hi):
            return slice(lo // GROUP, hi // GROUP)

        d_scale_table = keep.tile([P, G], U8, tag="d_scales_then_w1_scales", align_bytes=64)
        x_scale_table = keep.tile([P, T], U8, tag="x_scales_then_w1_words", align_bytes=64)
        placed_scales = keep.tile([P, H + S], U8, align_bytes=64)
        nc.gpsimd.memset(d_scale_table[:].bitcast(I32), 0)
        nc.vector.memset(x_scale_table[:].bitcast(I32), 0)
        nc.vector.memset(placed_scales[:].bitcast(I32), 0)

        kidx_sb = lists.tile([P, H // GROUP], U16)
        offs_sb = lists.tile([P, S // GROUP], U16)
        n1_sb = lists.tile([P, S // GROUP], U16)
        n2_sb = lists.tile([P, S // GROUP], U16)
        nc.sync.dma_start(kidx_sb[:], kidx)
        nc.sync.dma_start(offs_sb[:], offs)
        nc.sync.dma_start(n1_sb[:], n1)
        nc.sync.dma_start(n2_sb[:], n2)
        gain = keep.tile([P, PACK], F32)
        nc.sync.dma_start(d_scale_table[0:P:8, :].bitcast(I32), d_scales[0].bitcast(I32))
        nc.sync.dma_start(gain[:], gn.rearrange("(p t) o -> p (t o)", t=PACK))
        nc.sync.dma_start(x_scale_table[0:P:8, :].bitcast(I32), x_scales[0].bitcast(I32))
        d_table = keep.tile([P, G], I32, align_bytes=64)
        x_table = keep.tile([P, T], I32, align_bytes=64)
        nc.sync.dma_start(d_table[:], as_words(d_words))
        nc.sync.dma_start(x_table[:], as_words(x_words))

        picked_scales = keep.tile([P, H + S], U8, align_bytes=64)
        nc.vector.tensor_copy(picked_scales[:, 0:H], d_scale_table[:].indirect(kidx_sb[:]))
        nc.vector.tensor_copy(picked_scales[:, H : H + S], x_scale_table[:].indirect(offs_sb[:]))
        for q in range(QUADS):
            queue = nc.scalar if q % 2 else nc.sync
            queue.dma_start(
                placed_scales[32 * q : 32 * q + 4, :].bitcast(I32),
                picked_scales[32 * q : 32 * q + 32 : 8, :].bitcast(I32),
            )

        w1_table = keep.tile([P, N], I32, tag="x_scales_then_w1_words", align_bytes=64)
        nc.sync.dma_start(w1_table[:], as_words(w1_words))
        w1_scale_table = keep.tile([P, N], U8, tag="d_scales_then_w1_scales", align_bytes=64)
        nc.gpsimd.memset(w1_scale_table[:].bitcast(I32), 0)
        for q in range(QUADS):
            nc.sync.dma_start(
                w1_scale_table[32 * q : 32 * q + 4, :].bitcast(I32), w1_scales[0, 4 * q : 4 * q + 4, :].bitcast(I32)
            )

        d_picked = keep.tile([P, H], U32, align_bytes=64)
        nc.vector.tensor_copy(d_picked[:], d_table[:].bitcast(U32).indirect(kidx_sb[:]))
        d_codes = keep.tile([P, H], I32, align_bytes=64)
        nc.vector.tensor_copy(by_set(d_codes[:]), by_column(d_picked[:].bitcast(I32)))
        x_codes = keep.tile([P, S], U32, align_bytes=64)
        d_plane = keep.tile([P, H], U8, align_bytes=64)
        nc.vector.tensor_copy(x_codes[:, 0:HALF], x_table[:].bitcast(U32).indirect(offs_sb[:, entries(0, HALF)]))
        nc.vector.tensor_copy(by_set(d_plane[:]), by_column(placed_scales[:, 0:H]))
        nc.vector.tensor_copy(x_codes[:, HALF:S], x_table[:].bitcast(U32).indirect(offs_sb[:, entries(HALF, S)]))

        rival, own, second_halves = [], [], []
        for t in range(PACK):
            stationary = slice(t * P, (t + 1) * P)
            rival.append(keep.tile([P, S], F32, name=f"rival{t}"))
            own.append(keep.tile([P, S], F32, name=f"own{t}"))
            for lo, hi in ((0, HALF), (HALF, S)) if t == 0 else ((0, S),):
                bank = psum.tile([P, hi - lo], F32, name=f"score_bank{t}_{lo}", tag=f"bank{t}_{lo}")
                nc.tensor.matmul_mx(
                    out=bank[:],
                    lhsT=d_codes[:, stationary].bitcast(FP8X4),
                    lhsT_scale=d_plane[:, stationary],
                    rhs=x_codes[:, lo:hi].bitcast(FP8X4),
                    rhs_scale=placed_scales[:, H + lo : H + hi],
                    start=True,
                    stop=True,
                )
                nc.scalar.activation(rival[t][:, lo:hi], bank[:], ACT.Copy, scale=-0.5 * SCALE)
                if lo == 0:
                    nc.scalar.activation(own[t][:, 0:HALF], bank[:, 0:HALF], ACT.Copy, scale=SCALE)
                if hi == S:
                    second_halves.append(bank[:, HALF - lo : S - lo])
        for t in range(PACK):
            nc.scalar.activation(own[t][:, HALF:S], second_halves[t], ACT.Copy, scale=SCALE)

        w1_codes = keep.tile([P, N], I32, align_bytes=64)
        nc.vector.tensor_copy(by_set(w1_codes[:]), by_column(w1_table[:]))
        w1_plane = keep.tile([P, N], U8, align_bytes=64)
        nc.vector.tensor_copy(by_set(w1_plane[:]), by_column(w1_scale_table[:]))

        z_codes = keep.tile([P, S], U32, align_bytes=64)
        z_plane = keep.tile([P, S], U8, align_bytes=64)
        out_codes = keep.tile([P, S], U32, align_bytes=64)
        out_plane = keep.tile([P, S], U8, align_bytes=64)
        out_rows = out_0.rearrange("(p t) j -> p t j", t=PACK)
        out_words = as_words(out_1)

        widest = max(width for first_column, width in CHUNKS)
        ring_n1 = keep.tile([P, 2, widest], F32)
        ring_n2 = keep.tile([P, 2, widest], F32)
        last = len(CHUNKS) - 1
        z_sets = [
            keep.tile([P, PACK, width], BF16, name=f"z_sets{c}", align_bytes=64)
            for c, (first_column, width) in enumerate(CHUNKS)
        ]
        steps = [(c, t) for c in range(len(CHUNKS)) for t in range(PACK)]
        margin_n1, z_woven, out_woven = {}, {}, {}

        def columns(c):
            first_column, width = CHUNKS[c]
            return slice(first_column, first_column + width), width

        def fetch_n1(u):
            c, t = steps[u]
            cols, width = columns(c)
            if (c, t) in QUANTISE_AT:
                tag = f"z_woven{QUANTISE_AT[(c, t)]}"
                margin_n1[u] = keep.tile([P, width], F32, name=f"margin{u}", tag=tag, align_bytes=64)[:]
            else:
                margin_n1[u] = ring_n1[:, u % 2, 0:width]
            picked = rival[t][:].indirect(n1_sb[:, entries(cols.start, cols.stop)])
            nc.vector.tensor_tensor(margin_n1[u], picked, own[t][:, cols], ALU.add)

        def fetch_n2(u):
            c, t = steps[u]
            cols, width = columns(c)
            picked = rival[t][:].indirect(n2_sb[:, entries(cols.start, cols.stop)])
            nc.vector.tensor_tensor(ring_n2[:, u % 2, 0:width], picked, own[t][:, cols], ALU.add)

        def take_lesser(u):
            c, t = steps[u]
            cols, width = columns(c)
            margin_n2 = ring_n2[:, u % 2, 0:width]
            nc.vector.tensor_tensor(margin_n2, margin_n1[u], margin_n2, ALU.min)

        def weigh(u):
            c, t = steps[u]
            cols, width = columns(c)
            lesser = ring_n2[:, u % 2, 0:width]
            nc.vector.tensor_scalar(z_sets[c][:, t, :], lesser, 0.0, gain[:, t : t + 1], ALU.max, ALU.mult)
            if t == PACK - 1:
                z_woven[c] = keep.tile([P, width * PACK], BF16, name=f"z_woven{c}", tag=f"z_woven{c}", align_bytes=64)
                weave(nc.vector.tensor_copy if c == last else nc.scalar.copy, z_woven[c][:], z_sets[c][:])

        def second_product(c):
            cols, width = columns(c)
            nc.vector.quantize_mx(out=z_codes[:, cols].bitcast(FP8X4), scales=z_plane[:, cols], in_=z_woven[c][:])
            result = keep.tile([P, PACK, width], F32, name=f"result{c}")
            out_woven[c] = keep.tile([P, width * PACK], BF16, name=f"out_woven{c}", align_bytes=64)
            for lo in range(0, width, SUB):
                moving = slice(cols.start + lo, cols.start + lo + SUB)
                for t_lo, t_hi in ((0, 2), (2, 4)) if c == last else ((0, PACK),):
                    tag = f"bank{t_lo // 2}_0" if c == last else f"out_bank{moving.start}"
                    bank = psum.tile([P, t_hi - t_lo, SUB], F32, name=f"out_bank{moving.start}_{t_lo}", tag=tag)
                    for t in range(t_lo, t_hi):
                        stationary = slice(t * P, (t + 1) * P)
                        nc.tensor.matmul_mx(
                            out=bank[:, t - t_lo, :],
                            lhsT=w1_codes[:, stationary].bitcast(FP8X4),
                            lhsT_scale=w1_plane[:, stationary],
                            rhs=z_codes[:, moving].bitcast(FP8X4),
                            rhs_scale=z_plane[:, moving],
                            start=True,
                            stop=True,
                        )
                    nc.scalar.copy(result[:, t_lo:t_hi, lo : lo + SUB], bank[:])
                target = out_woven[c][:, lo * PACK : (lo + SUB) * PACK]
                if c == last:
                    weave(nc.vector.tensor_copy, target, result[:])
                else:
                    nc.scalar.copy(target.rearrange("p (j t) -> p j t", t=PACK), bank[:].rearrange("p t j -> p j t"))
            nc.sync.dma_start(out_rows[:, :, cols], result[:])

        def hand_on(c):
            cols, width = columns(c)
            nc.vector.quantize_mx(out=out_codes[:, cols].bitcast(FP8X4), scales=out_plane[:, cols], in_=out_woven[c][:])
            nc.sync.dma_start(out_words[:, cols], out_codes[:, cols].bitcast(I32))

        for u in range(len(steps) + 1):
            if u < len(steps):
                if steps[u] in QUANTISE_AT:
                    second_product(QUANTISE_AT[steps[u]])
                fetch_n1(u)
            else:
                hand_on(0)
            if u > 0:
                take_lesser(u - 1)
            if u < len(steps):
                fetch_n2(u)
            if u > 0:
                weigh(u - 1)
        second_product(last)
        hand_on(last - 1)
        hand_on(last)
        for q in range(QUADS):
            queue = nc.scalar if q % 2 else nc.sync
            queue.dma_start(out_2[0, 4 * q : 4 * q + 4, :].bitcast(I32), out_plane[32 * q : 32 * q + 4, :].bitcast(I32))
